import numpy as np
import ml_dtypes


def mxq(x, axis, fmt="e4m3"):
    dtype, down = {"e4m3": (ml_dtypes.float8_e4m3fn, 7), "e5m2": (ml_dtypes.float8_e5m2, 14)}[fmt]
    v = np.moveaxis(np.asarray(x, np.float32).astype(ml_dtypes.bfloat16).astype(np.float64), axis, -1)
    blocks = v.reshape(v.shape[:-1] + (-1, 32))
    amax = np.abs(blocks).max(-1, keepdims=True)
    byte = np.maximum(np.where(amax > 0, np.frexp(amax)[1] - 1 + 127, 0) - down, 1)
    scale = np.exp2(byte - 127.0)
    codes = (blocks / scale).astype(np.float32).astype(dtype).astype(np.float64)
    return np.moveaxis((codes * scale).reshape(v.shape), -1, axis)


WIDE = False


def mx_kscale(k):
    if not WIDE:
        return np.ones(k)
    levels = np.array([10, -10, 5, -5, 0])
    if k % 512:
        return np.exp2(np.random.permutation(np.resize(levels, k // 32))).repeat(32)
    a = np.empty((k // 512, 16))
    for p in range(k // 512):
        a[p, :8] = np.random.permutation(np.resize(levels, 8))
        for g in range(8):
            far = levels[np.abs(levels - a[p, g]) >= 10]
            a[p, g + 8] = far[np.random.randint(len(far))]
    return np.exp2(a.ravel()).repeat(32)


def f64(x):
    return np.asarray(x).astype(np.float64)


def striped(idx):
    return np.tile(idx.reshape(-1, 16).T, (8, 1)).astype(np.uint16)


def unstriped(offs):
    return offs[:16].T.reshape(-1).astype(np.int64)


def d_relu2(v):
    return 2.0 * np.maximum(v, 0.0)


K, T, E, C, H, N = 128, 1024, 2, 512, 1024, 512


def by_expert(wq, xq):
    return np.concatenate([wq[e].T @ xq[:, e * C:(e + 1) * C] for e in range(E)], axis=1)


def setup_inputs():
    n = np.random.standard_normal
    slot_token = np.random.permutation(T)[:E * C]
    s = mx_kscale(N)[:, None]
    z = np.ones(T); z[slot_token] = mx_kscale(E * C)
    return {
        "xT": (n((K, T)) * z[None, :]).astype(np.float32),
        "dyT": (n((N, T)) * s).astype(np.float32),
        "a": n((H, E * C)).astype(np.float32),
        "w2": (n((E, N, H)) / np.sqrt(N) / s[None]).astype(np.float32),
        "gate": np.tile(np.random.uniform(0.2, 1.0, E * C) / z[slot_token], (N, 1)).astype(np.float32),
        "offs": striped(slot_token),
    }


def reference(xT, dyT, a, w2, gate, offs):
    idx = unstriped(offs)
    gq = mxq(f64(gate) * f64(dyT)[:, idx], 0, "e4m3")
    dh = by_expert(mxq(f64(w2), 1, "e4m3"), gq)
    da = mxq(dh * d_relu2(f64(a)), 1, "e4m3")
    xq = mxq(f64(xT)[:, idx], 1, "e4m3")
    return np.stack([(xq[:, e * C:(e + 1) * C] @ da[:, e * C:(e + 1) * C].T) for e in range(E)])

@@ -1,0 +1,241 @@
+from contextlib import ExitStack
+
+import concourse.mybir as mybir
+from concourse.masks import make_identity
+
+K, T, E, C, H, N = 128, 1024, 2, 512, 1024, 512
+FLOPS = 2 * E * C * H * (N + K)
+BYTES = 4 * (K * T + N * T + H * E * C + E * N * H + E * C + E * K * H) + 2 * 128 * 64
+
+F32 = mybir.dt.float32
+BF16 = mybir.dt.bfloat16
+U32 = mybir.dt.uint32
+U16 = mybir.dt.uint16
+U8 = mybir.dt.uint8
+FP8X4 = mybir.dt.float8_e4m3fn_x4
+ALU = mybir.AluOpType
+COPY = mybir.ActivationFunctionType.Copy
+
+P = 128
+PACK = 4
+CHUNK = 256
+CHUNKS = H // CHUNK
+HALF = C // 2
+LIST_COLS = C // 16
+
+
+def tile_moe_mlp_relu2_kernel(tc, xT, dyT, a, w2, gate, offs, out):
+    nc = tc.nc
+    with ExitStack() as ctx:
+        keep = ctx.enter_context(tc.tile_pool(name="keep", bufs=1))
+        ring = ctx.enter_context(tc.tile_pool(name="ring", bufs=3))
+        psum = ctx.enter_context(tc.psum_pool(name="psum", bufs=2))
+
+        offsets = keep.tile([P, E * LIST_COLS], U16, name="offsets")
+        gates = [keep.tile([P, C], F32, name=f"gate{e}") for e in range(E)]
+        dy = [keep.tile([P, T], F32, name=f"dy{t}") for t in range(PACK)]
+        x_f32 = keep.tile([P, T], F32, name="x_f32")
+        w_raw = {}
+        a_raw = {(e, c): keep.tile([P, 2 * C], F32, name=f"a_raw{e}{c}") for e in range(E) for c in range(CHUNKS)}
+        dy_rows = dyT.rearrange("(p t) j -> p t j", t=PACK)
+
+        def load_w(e, c, chunks):
+            tile = keep.tile([P, PACK, chunks * CHUNK], F32, name=f"w_raw{e}{c}")
+            nc.sync.dma_start(tile[:], w2[e].rearrange("(p t) i -> p t i", t=PACK)[:, :, c * CHUNK : (c + chunks) * CHUNK])
+            for d in range(chunks):
+                w_raw[e, c + d] = tile[:, :, d * CHUNK : (d + 1) * CHUNK]
+
+        def load_a(e, c):
+            rows = a[c * CHUNK : (c + 1) * CHUNK, e * C : (e + 1) * C]
+            nc.sync.dma_start(a_raw[e, c][:].rearrange("p (m j) -> p m j", m=2), rows.rearrange("(m p) j -> p m j", m=2))
+
+        nc.sync.dma_start(offsets[:], offs)
+        nc.sync.dma_start(gates[0][:], gate[0:P, 0:C])
+        nc.sync.dma_start(dy[0][:], dy_rows[:, 0, :])
+        nc.sync.dma_start(gates[1][:], gate[0:P, C : 2 * C])
+        nc.sync.dma_start(x_f32[:], xT)
+        nc.sync.dma_start(dy[1][:], dy_rows[:, 1, :])
+        load_w(0, 0, 1)
+        nc.sync.dma_start(dy[2][:], dy_rows[:, 2, :])
+        load_w(0, 1, 1)
+        nc.sync.dma_start(dy[3][:], dy_rows[:, 3, :])
+        load_a(0, 0)
+        load_w(0, 2, 2)
+        load_a(0, 1)
+        load_a(0, 2)
+        load_w(1, 0, 2)
+        load_a(0, 3)
+        load_a(1, 0)
+        load_w(1, 2, 2)
+        load_a(1, 1)
+        load_a(1, 2)
+        load_a(1, 3)
+
+        ident = keep.tile([P, P], F32, name="ident")
+        make_identity(nc, ident[:])
+
+        def slot_list(e):
+            return offsets[:, e * LIST_COLS : (e + 1) * LIST_COLS]
+
+        g_f32 = [keep.tile([P, PACK, C], F32, name=f"g_f32{e}") for e in range(E)]
+        for t in range(PACK):
+            for e in range(E):
+                nc.vector.tensor_tensor(g_f32[e][:, t, :], dy[t][:].indirect(slot_list(e)), gates[e][:], ALU.mult)
+
+        def quantize(codes, scales, values):
+            nc.vector.quantize_mx(out=codes.bitcast(FP8X4), scales=scales, in_=values)
+
+        def turn(source, blocks):
+            bank = psum.tile([P, len(blocks), 2, P], F32, name="turned")
+            words = source[:].bitcast(F32)
+            for place, m in enumerate(blocks):
+                for u in range(2):
+                    first = (2 * u + m) * P
+                    nc.tensor.transpose(bank[:, place, u, :], words[:, first : first + P], ident[:])
+            return bank
+
+        def weave(bank, name, copy):
+            blocks = bank.shape[1]
+            woven = ring.tile([P, blocks * P * PACK], BF16, name=name, align_bytes=64)
+            copy(woven[:].bitcast(F32).rearrange("p (m i u) -> p m i u", m=blocks, u=2), bank[:].rearrange("p m u i -> p m i u"))
+            return woven
+
+        x_bf = keep.tile([P, T], BF16, name="x_bf")
+        nc.scalar.activation(x_bf[:], x_f32[:], COPY)
+        x_slots = keep.tile([P, E * C], BF16, name="x_slots", align_bytes=64)
+        for e in range(E):
+            view = x_slots[:].rearrange("p (u e b s) -> p e b u s", u=2, e=E, s=16)[:, e]
+            nc.scalar.activation(view, x_bf[:].indirect(slot_list(e)), COPY)
+        x_woven = weave(turn(x_slots, (0, 1)), "x_woven", nc.scalar.copy)
+        x_codes = keep.tile([P, E * K], U32, name="x_codes", align_bytes=64)
+        x_scales = keep.tile([P, E * K], U8, name="x_scales", align_bytes=64)
+
+        w_bf, w_q = {}, {}
+
+        def round_w(e, c):
+            tile = ring.tile([P, CHUNK * PACK], BF16, name="w_bf", align_bytes=64)
+            source = w_raw[e, c]
+            copy = nc.vector.tensor_copy if (e, c) in () else nc.scalar.copy
+            copy(tile[:].rearrange("p (c i t) -> p c t i", i=4, t=PACK), source.rearrange("p t (c i) -> p c t i", i=4))
+            w_bf[e, c] = tile
+
+        def quantize_w(e, c):
+            codes = ring.tile([P, CHUNK], U32, name="w_codes", align_bytes=64)
+            scales = ring.tile([P, CHUNK], U8, name="w_scales", align_bytes=64)
+            quantize(codes[:], scales[:], w_bf[e, c][:])
+            w_q[e, c] = (codes, scales)
+
+        g_bf, g_q = {}, {}
+
+        def round_g(e, u):
+            tile = keep.tile([P, HALF * PACK], BF16, name=f"g_bf{e}{u}", align_bytes=64)
+            source = g_f32[e][:].rearrange("p t (b u c i) -> p u b c t i", u=2, c=4, i=4)[:, u]
+            copy = nc.vector.tensor_copy if (e, u) in ((0, 1),) else nc.scalar.copy
+            copy(tile[:].rearrange("p (b c i t) -> p b c t i", c=4, i=4, t=PACK), source)
+            g_bf[e, u] = tile
+
+        def quantize_g(e, u):
+            codes = keep.tile([P, HALF], U32, name=f"g_codes{e}{u}", align_bytes=64)
+            scales = keep.tile([P, HALF], U8, name=f"g_scales{e}{u}", align_bytes=64)
+            quantize(codes[:], scales[:], g_bf[e, u][:])
+            g_q[e, u] = (codes, scales)
+
+        da_tiles = {}
+
+        def first_product(e, c):
+            w_codes, w_scales = w_q[e, c]
+            banks = []
+            for u in range(2):
+                g_codes, g_scales = g_q[e, u]
+                dh = psum.tile([P, 2 * HALF], F32, name=f"dh{u}")
+                for m in range(2):
+                    cols = slice(m * P, (m + 1) * P)
+                    nc.tensor.matmul_mx(
+                        out=dh[:, m * HALF : (m + 1) * HALF],
+                        lhsT=w_codes[:, cols].bitcast(FP8X4),
+                        lhsT_scale=w_scales[:, cols],
+                        rhs=g_codes[:].bitcast(FP8X4),
+                        rhs_scale=g_scales[:],
+                        start=True,
+                        stop=True,
+                    )
+                banks.append(dh)
+            da = ring.tile([P, 2 * C], BF16, name="da", align_bytes=64)
+            da_tiles[e, c] = (da, banks)
+
+        def make_da(e, c, blocks):
+            da, banks = da_tiles[e, c]
+            runs = slice(16 * blocks[0], 16 * (blocks[-1] + 1))
+            for u in range(2):
+                nc.vector.scalar_tensor_tensor(
+                    da[:].rearrange("p (u r s) -> p u r s", u=2, s=16)[:, u, runs],
+                    a_raw[e, c][:].rearrange("p (r u s) -> p u r s", u=2, s=16)[:, u, runs],
+                    0.0,
+                    banks[u][:].rearrange("p (r s) -> p r s", s=16)[:, runs],
+                    ALU.max,
+                    ALU.mult,
+                )
+
+        woven_da = {}
+
+        def turn_da(e, c, blocks, copy):
+            woven_da[e, c, blocks] = weave(turn(da_tiles[e, c][0], blocks), "da_woven", copy)
+
+        def second_product(e, c, blocks, on_vector):
+            width = len(blocks) * P
+            codes = ring.tile([P, width], U32, name="da_codes", align_bytes=64)
+            scales = ring.tile([P, width], U8, name="da_scales", align_bytes=64)
+            quantize(codes[:], scales[:], woven_da[e, c, blocks][:])
+            acc = psum.tile([P, width], F32, name="acc")
+            cols = slice(e * K, (e + 1) * K)
+            nc.tensor.matmul_mx(
+                out=acc[:],
+                lhsT=x_codes[:, cols].bitcast(FP8X4),
+                lhsT_scale=x_scales[:, cols],
+                rhs=codes[:].bitcast(FP8X4),
+                rhs_scale=scales[:],
+                start=True,
+                stop=True,
+            )
+            result = keep.tile([P, width], F32, name=f"result{e}{c}{blocks[0]}")
+            if on_vector:
+                nc.vector.tensor_scalar_mul(result[:], acc[:], 2.0)
+            else:
+                nc.scalar.activation(result[:], acc[:], COPY, scale=2.0)
+            first = c * CHUNK + blocks[0] * P
+            nc.sync.dma_start(out[e][:, first : first + width], result[:])
+
+        steps = [(e, c) for e in range(E) for c in range(CHUNKS)]
+        both = (0, 1)
+        last = len(steps) - 1
+        round_w(*steps[0])
+        round_w(*steps[1])
+        quantize_w(*steps[0])
+        for u in range(2):
+            round_g(0, u)
+            quantize_g(0, u)
+        quantize_w(*steps[1])
+        quantize(x_codes[:], x_scales[:], x_woven[:])
+        for s in range(last):
+            first_product(*steps[s])
+            make_da(*steps[s], both)
+            if s >= 2:
+                second_product(*steps[s - 2], both, False)
+            if s >= 1:
+                turn_da(*steps[s - 1], both, nc.scalar.copy)
+            if s + 2 <= last:
+                round_w(*steps[s + 2])
+                quantize_w(*steps[s + 2])
+            if 1 <= s < 3:
+                round_g(1, s - 1)
+                quantize_g(1, s - 1)
+        first_product(*steps[last])
+        make_da(*steps[last], (0,))
+        second_product(*steps[last - 2], both, False)
+        turn_da(*steps[last - 1], both, nc.scalar.copy)
+        make_da(*steps[last], (1,))
+        turn_da(*steps[last], (0,), nc.scalar.copy)
+        second_product(*steps[last - 1], both, False)
+        turn_da(*steps[last], (1,), nc.scalar.copy)
+        second_product(*steps[last], (0,), False)
+        second_product(*steps[last], (1,), True)

@@ -36,7 +36,7 @@ def tile_moe_mlp_relu2_kernel(tc, xT, dyT, a, w2, gate, offs, out):
         dy = [keep.tile([P, T], F32, name=f"dy{t}") for t in range(PACK)]
         x_f32 = keep.tile([P, T], F32, name="x_f32")
         w_raw = {}
-        a_raw = {(e, c): keep.tile([P, 2 * C], F32, name=f"a_raw{e}{c}") for e in range(E) for c in range(CHUNKS)}
+        a_raw = {}
         dy_rows = dyT.rearrange("(p t) j -> p t j", t=PACK)
 
         def load_w(e, c, chunks):
@@ -45,34 +45,45 @@ def tile_moe_mlp_relu2_kernel(tc, xT, dyT, a, w2, gate, offs, out):
             for d in range(chunks):
                 w_raw[e, c + d] = tile[:, :, d * CHUNK : (d + 1) * CHUNK]
 
-        def load_a(e, c):
-            rows = a[c * CHUNK : (c + 1) * CHUNK, e * C : (e + 1) * C]
-            nc.sync.dma_start(a_raw[e, c][:].rearrange("p (m j) -> p m j", m=2), rows.rearrange("(m p) j -> p m j", m=2))
+        def load_a(e, c, blocks=(0, 1)):
+            tile = keep.tile([P, len(blocks) * C], F32, name=f"a_raw{e}{c}{blocks[0]}")
+            rows = a[c * CHUNK + blocks[0] * P : c * CHUNK + (blocks[-1] + 1) * P, e * C : (e + 1) * C]
+            nc.sync.dma_start(tile[:].rearrange("p (m j) -> p m j", m=len(blocks)), rows.rearrange("(m p) j -> p m j", p=P))
+            a_raw[e, c, blocks] = tile
 
+        gate_cols = [keep.tile([P, PACK], F32, name=f"gate_cols{e}") for e in range(E)]
+        for e in range(E):
+            nc.sync.dma_start(gate_cols[e][:], gate[0:1, e * C : (e + 1) * C].rearrange("o (q c) -> (o q) c", c=PACK))
         nc.sync.dma_start(offsets[:], offs)
-        nc.sync.dma_start(gates[0][:], gate[0:P, 0:C])
         nc.sync.dma_start(dy[0][:], dy_rows[:, 0, :])
-        nc.sync.dma_start(gates[1][:], gate[0:P, C : 2 * C])
         nc.sync.dma_start(x_f32[:], xT)
         nc.sync.dma_start(dy[1][:], dy_rows[:, 1, :])
-        load_w(0, 0, 1)
         nc.sync.dma_start(dy[2][:], dy_rows[:, 2, :])
-        load_w(0, 1, 1)
+        load_w(0, 0, 2)
         nc.sync.dma_start(dy[3][:], dy_rows[:, 3, :])
         load_a(0, 0)
         load_w(0, 2, 2)
         load_a(0, 1)
-        load_a(0, 2)
         load_w(1, 0, 2)
+        load_a(0, 2)
         load_a(0, 3)
-        load_a(1, 0)
         load_w(1, 2, 2)
+        load_a(1, 0)
         load_a(1, 1)
         load_a(1, 2)
-        load_a(1, 3)
+        load_a(1, 3, (0,))
+        load_a(1, 3, (1,))
 
         ident = keep.tile([P, P], F32, name="ident")
         make_identity(nc, ident[:])
+
+        for e in (0, 1):
+            wide = keep.tile([P, PACK, P], F32, name=f"gate_wide{e}", tag=f"wide{e}")
+            nc.vector.tensor_copy(wide[:], gate_cols[e][:].unsqueeze(2).to_broadcast([P, PACK, P]))
+            bank = psum.tile([P, PACK, P], F32, name="acc")
+            for c in range(PACK):
+                nc.tensor.transpose(bank[:, c, :], wide[:, c, :], ident[:])
+            nc.scalar.activation(gates[e][:].rearrange("p (q c) -> p q c", c=PACK), bank[:].rearrange("p c q -> p q c"), COPY)
 
         def slot_list(e):
             return offsets[:, e * LIST_COLS : (e + 1) * LIST_COLS]
@@ -100,7 +111,7 @@ def tile_moe_mlp_relu2_kernel(tc, xT, dyT, a, w2, gate, offs, out):
             copy(woven[:].bitcast(F32).rearrange("p (m i u) -> p m i u", m=blocks, u=2), bank[:].rearrange("p m u i -> p m i u"))
             return woven
 
-        x_bf = keep.tile([P, T], BF16, name="x_bf")
+        x_bf = keep.tile([P, T], BF16, name="x_bf", tag="wide1")
         nc.scalar.activation(x_bf[:], x_f32[:], COPY)
         x_slots = keep.tile([P, E * C], BF16, name="x_slots", align_bytes=64)
         for e in range(E):
@@ -120,8 +131,8 @@ def tile_moe_mlp_relu2_kernel(tc, xT, dyT, a, w2, gate, offs, out):
             w_bf[e, c] = tile
 
         def quantize_w(e, c):
-            codes = ring.tile([P, CHUNK], U32, name="w_codes", align_bytes=64)
-            scales = ring.tile([P, CHUNK], U8, name="w_scales", align_bytes=64)
+            codes = keep.tile([P, CHUNK], U32, name=f"w_codes{e}{c}", align_bytes=64)
+            scales = keep.tile([P, CHUNK], U8, name=f"w_scales{e}{c}", align_bytes=64)
             quantize(codes[:], scales[:], w_bf[e, c][:])
             w_q[e, c] = (codes, scales)
 
@@ -130,7 +141,7 @@ def tile_moe_mlp_relu2_kernel(tc, xT, dyT, a, w2, gate, offs, out):
         def round_g(e, u):
             tile = keep.tile([P, HALF * PACK], BF16, name=f"g_bf{e}{u}", align_bytes=64)
             source = g_f32[e][:].rearrange("p t (b u c i) -> p u b c t i", u=2, c=4, i=4)[:, u]
-            copy = nc.vector.tensor_copy if (e, u) in ((0, 1),) else nc.scalar.copy
+            copy = nc.vector.tensor_copy if (e, u) in ((0, 1), (1, 1)) else nc.scalar.copy
             copy(tile[:].rearrange("p (b c i t) -> p b c t i", c=4, i=4, t=PACK), source)
             g_bf[e, u] = tile
 
@@ -169,7 +180,7 @@ def tile_moe_mlp_relu2_kernel(tc, xT, dyT, a, w2, gate, offs, out):
             for u in range(2):
                 nc.vector.scalar_tensor_tensor(
                     da[:].rearrange("p (u r s) -> p u r s", u=2, s=16)[:, u, runs],
-                    a_raw[e, c][:].rearrange("p (r u s) -> p u r s", u=2, s=16)[:, u, runs],
+                    a_raw[e, c, blocks][:].rearrange("p (r u s) -> p u r s", u=2, s=16)[:, u],
                     0.0,
                     banks[u][:].rearrange("p (r s) -> p r s", s=16)[:, runs],
                     ALU.max,
@@ -226,9 +237,9 @@ def tile_moe_mlp_relu2_kernel(tc, xT, dyT, a, w2, gate, offs, out):
             if s + 2 <= last:
                 round_w(*steps[s + 2])
                 quantize_w(*steps[s + 2])
-            if 1 <= s < 3:
-                round_g(1, s - 1)
-                quantize_g(1, s - 1)
+            if 0 <= s < 2:
+                round_g(1, s - 0)
+                quantize_g(1, s - 0)
         first_product(*steps[last])
         make_da(*steps[last], (0,))
         second_product(*steps[last - 2], both, False)
@@ -238,4 +249,4 @@ def tile_moe_mlp_relu2_kernel(tc, xT, dyT, a, w2, gate, offs, out):
         second_product(*steps[last - 1], both, False)
         turn_da(*steps[last], (1,), nc.scalar.copy)
         second_product(*steps[last], (0,), False)
-        second_product(*steps[last], (1,), True)
+        second_product(*steps[last], (1,), False)

from contextlib import ExitStack

import concourse.mybir as mybir
from concourse.masks import make_identity

K, T, E, C, H, N = 128, 1024, 2, 512, 1024, 512
FLOPS = 2 * E * C * H * (N + K)
BYTES = 4 * (K * T + N * T + H * E * C + E * N * H + E * C + E * K * H) + 2 * 128 * 64

F32 = mybir.dt.float32
BF16 = mybir.dt.bfloat16
U32 = mybir.dt.uint32
U16 = mybir.dt.uint16
U8 = mybir.dt.uint8
FP8X4 = mybir.dt.float8_e4m3fn_x4
ALU = mybir.AluOpType
COPY = mybir.ActivationFunctionType.Copy

P = 128
PACK = 4
CHUNK = 256
CHUNKS = H // CHUNK
HALF = C // 2
LIST_COLS = C // 16


def tile_moe_mlp_relu2_kernel(tc, xT, dyT, a, w2, gate, offs, out):
    nc = tc.nc
    with ExitStack() as ctx:
        keep = ctx.enter_context(tc.tile_pool(name="keep", bufs=1))
        ring = ctx.enter_context(tc.tile_pool(name="ring", bufs=3))
        psum = ctx.enter_context(tc.psum_pool(name="psum", bufs=2))

        offsets = keep.tile([P, E * LIST_COLS], U16, name="offsets")
        gates = [keep.tile([P, C], F32, name=f"gate{e}") for e in range(E)]
        dy = [keep.tile([P, T], F32, name=f"dy{t}") for t in range(PACK)]
        x_f32 = keep.tile([P, T], F32, name="x_f32")
        w_raw = {}
        a_raw = {}
        dy_rows = dyT.rearrange("(p t) j -> p t j", t=PACK)

        def load_w(e, c, chunks):
            tile = keep.tile([P, PACK, chunks * CHUNK], F32, name=f"w_raw{e}{c}")
            nc.sync.dma_start(tile[:], w2[e].rearrange("(p t) i -> p t i", t=PACK)[:, :, c * CHUNK : (c + chunks) * CHUNK])
            for d in range(chunks):
                w_raw[e, c + d] = tile[:, :, d * CHUNK : (d + 1) * CHUNK]

        def load_a(e, c, blocks=(0, 1)):
            tile = keep.tile([P, len(blocks) * C], F32, name=f"a_raw{e}{c}{blocks[0]}")
            rows = a[c * CHUNK + blocks[0] * P : c * CHUNK + (blocks[-1] + 1) * P, e * C : (e + 1) * C]
            nc.sync.dma_start(tile[:].rearrange("p (m j) -> p m j", m=len(blocks)), rows.rearrange("(m p) j -> p m j", p=P))
            a_raw[e, c, blocks] = tile

        gate_cols = [keep.tile([P, PACK], F32, name=f"gate_cols{e}") for e in range(E)]
        for e in range(E):
            nc.sync.dma_start(gate_cols[e][:], gate[0:1, e * C : (e + 1) * C].rearrange("o (q c) -> (o q) c", c=PACK))
        nc.sync.dma_start(offsets[:], offs)
        nc.sync.dma_start(dy[0][:], dy_rows[:, 0, :])
        nc.sync.dma_start(x_f32[:], xT)
        nc.sync.dma_start(dy[1][:], dy_rows[:, 1, :])
        nc.sync.dma_start(dy[2][:], dy_rows[:, 2, :])
        load_w(0, 0, 2)
        nc.sync.dma_start(dy[3][:], dy_rows[:, 3, :])
        load_a(0, 0)
        load_w(0, 2, 2)
        load_a(0, 1)
        load_w(1, 0, 2)
        load_a(0, 2)
        load_a(0, 3)
        load_w(1, 2, 2)
        load_a(1, 0)
        load_a(1, 1)
        load_a(1, 2)
        load_a(1, 3, (0,))
        load_a(1, 3, (1,))

        ident = keep.tile([P, P], F32, name="ident")
        make_identity(nc, ident[:])

        for e in (0, 1):
            wide = keep.tile([P, PACK, P], F32, name=f"gate_wide{e}", tag=f"wide{e}")
            nc.vector.tensor_copy(wide[:], gate_cols[e][:].unsqueeze(2).to_broadcast([P, PACK, P]))
            bank = psum.tile([P, PACK, P], F32, name="acc")
            for c in range(PACK):
                nc.tensor.transpose(bank[:, c, :], wide[:, c, :], ident[:])
            nc.scalar.activation(gates[e][:].rearrange("p (q c) -> p q c", c=PACK), bank[:].rearrange("p c q -> p q c"), COPY)

        def slot_list(e):
            return offsets[:, e * LIST_COLS : (e + 1) * LIST_COLS]

        g_f32 = [keep.tile([P, PACK, C], F32, name=f"g_f32{e}") for e in range(E)]
        for t in range(PACK):
            for e in range(E):
                nc.vector.tensor_tensor(g_f32[e][:, t, :], dy[t][:].indirect(slot_list(e)), gates[e][:], ALU.mult)

        def quantize(codes, scales, values):
            nc.vector.quantize_mx(out=codes.bitcast(FP8X4), scales=scales, in_=values)

        def turn(source, blocks):
            bank = psum.tile([P, len(blocks), 2, P], F32, name="turned")
            words = source[:].bitcast(F32)
            for place, m in enumerate(blocks):
                for u in range(2):
                    first = (2 * u + m) * P
                    nc.tensor.transpose(bank[:, place, u, :], words[:, first : first + P], ident[:])
            return bank

        def weave(bank, name, copy):
            blocks = bank.shape[1]
            woven = ring.tile([P, blocks * P * PACK], BF16, name=name, align_bytes=64)
            copy(woven[:].bitcast(F32).rearrange("p (m i u) -> p m i u", m=blocks, u=2), bank[:].rearrange("p m u i -> p m i u"))
            return woven

        x_bf = keep.tile([P, T], BF16, name="x_bf", tag="wide1")
        nc.scalar.activation(x_bf[:], x_f32[:], COPY)
        x_slots = keep.tile([P, E * C], BF16, name="x_slots", align_bytes=64)
        for e in range(E):
            view = x_slots[:].rearrange("p (u e b s) -> p e b u s", u=2, e=E, s=16)[:, e]
            nc.scalar.activation(view, x_bf[:].indirect(slot_list(e)), COPY)
        x_woven = weave(turn(x_slots, (0, 1)), "x_woven", nc.scalar.copy)
        x_codes = keep.tile([P, E * K], U32, name="x_codes", align_bytes=64)
        x_scales = keep.tile([P, E * K], U8, name="x_scales", align_bytes=64)

        w_bf, w_q = {}, {}

        def round_w(e, c):
            tile = ring.tile([P, CHUNK * PACK], BF16, name="w_bf", align_bytes=64)
            source = w_raw[e, c]
            copy = nc.vector.tensor_copy if (e, c) in () else nc.scalar.copy
            copy(tile[:].rearrange("p (c i t) -> p c t i", i=4, t=PACK), source.rearrange("p t (c i) -> p c t i", i=4))
            w_bf[e, c] = tile

        def quantize_w(e, c):
            codes = keep.tile([P, CHUNK], U32, name=f"w_codes{e}{c}", align_bytes=64)
            scales = keep.tile([P, CHUNK], U8, name=f"w_scales{e}{c}", align_bytes=64)
            quantize(codes[:], scales[:], w_bf[e, c][:])
            w_q[e, c] = (codes, scales)

        g_bf, g_q = {}, {}

        def round_g(e, u):
            tile = keep.tile([P, HALF * PACK], BF16, name=f"g_bf{e}{u}", align_bytes=64)
            source = g_f32[e][:].rearrange("p t (b u c i) -> p u b c t i", u=2, c=4, i=4)[:, u]
            copy = nc.vector.tensor_copy if (e, u) in ((0, 1), (1, 1)) else nc.scalar.copy
            copy(tile[:].rearrange("p (b c i t) -> p b c t i", c=4, i=4, t=PACK), source)
            g_bf[e, u] = tile

        def quantize_g(e, u):
            codes = keep.tile([P, HALF], U32, name=f"g_codes{e}{u}", align_bytes=64)
            scales = keep.tile([P, HALF], U8, name=f"g_scales{e}{u}", align_bytes=64)
            quantize(codes[:], scales[:], g_bf[e, u][:])
            g_q[e, u] = (codes, scales)

        da_tiles = {}

        def first_product(e, c):
            w_codes, w_scales = w_q[e, c]
            banks = []
            for u in range(2):
                g_codes, g_scales = g_q[e, u]
                dh = psum.tile([P, 2 * HALF], F32, name=f"dh{u}")
                for m in range(2):
                    cols = slice(m * P, (m + 1) * P)
                    nc.tensor.matmul_mx(
                        out=dh[:, m * HALF : (m + 1) * HALF],
                        lhsT=w_codes[:, cols].bitcast(FP8X4),
                        lhsT_scale=w_scales[:, cols],
                        rhs=g_codes[:].bitcast(FP8X4),
                        rhs_scale=g_scales[:],
                        start=True,
                        stop=True,
                    )
                banks.append(dh)
            da = ring.tile([P, 2 * C], BF16, name="da", align_bytes=64)
            da_tiles[e, c] = (da, banks)

        def make_da(e, c, blocks):
            da, banks = da_tiles[e, c]
            runs = slice(16 * blocks[0], 16 * (blocks[-1] + 1))
            for u in range(2):
                nc.vector.scalar_tensor_tensor(
                    da[:].rearrange("p (u r s) -> p u r s", u=2, s=16)[:, u, runs],
                    a_raw[e, c, blocks][:].rearrange("p (r u s) -> p u r s", u=2, s=16)[:, u],
                    0.0,
                    banks[u][:].rearrange("p (r s) -> p r s", s=16)[:, runs],
                    ALU.max,
                    ALU.mult,
                )

        woven_da = {}

        def turn_da(e, c, blocks, copy):
            woven_da[e, c, blocks] = weave(turn(da_tiles[e, c][0], blocks), "da_woven", copy)

        def second_product(e, c, blocks, on_vector):
            width = len(blocks) * P
            codes = ring.tile([P, width], U32, name="da_codes", align_bytes=64)
            scales = ring.tile([P, width], U8, name="da_scales", align_bytes=64)
            quantize(codes[:], scales[:], woven_da[e, c, blocks][:])
            acc = psum.tile([P, width], F32, name="acc")
            cols = slice(e * K, (e + 1) * K)
            nc.tensor.matmul_mx(
                out=acc[:],
                lhsT=x_codes[:, cols].bitcast(FP8X4),
                lhsT_scale=x_scales[:, cols],
                rhs=codes[:].bitcast(FP8X4),
                rhs_scale=scales[:],
                start=True,
                stop=True,
            )
            result = keep.tile([P, width], F32, name=f"result{e}{c}{blocks[0]}")
            if on_vector:
                nc.vector.tensor_scalar_mul(result[:], acc[:], 2.0)
            else:
                nc.scalar.activation(result[:], acc[:], COPY, scale=2.0)
            first = c * CHUNK + blocks[0] * P
            nc.sync.dma_start(out[e][:, first : first + width], result[:])

        steps = [(e, c) for e in range(E) for c in range(CHUNKS)]
        both = (0, 1)
        last = len(steps) - 1
        round_w(*steps[0])
        round_w(*steps[1])
        quantize_w(*steps[0])
        for u in range(2):
            round_g(0, u)
            quantize_g(0, u)
        quantize_w(*steps[1])
        quantize(x_codes[:], x_scales[:], x_woven[:])
        for s in range(last):
            first_product(*steps[s])
            make_da(*steps[s], both)
            if s >= 2:
                second_product(*steps[s - 2], both, False)
            if s >= 1:
                turn_da(*steps[s - 1], both, nc.scalar.copy)
            if s + 2 <= last:
                round_w(*steps[s + 2])
                quantize_w(*steps[s + 2])
            if 0 <= s < 2:
                round_g(1, s - 0)
                quantize_g(1, s - 0)
        first_product(*steps[last])
        make_da(*steps[last], (0,))
        second_product(*steps[last - 2], both, False)
        turn_da(*steps[last - 1], both, nc.scalar.copy)
        make_da(*steps[last], (1,))
        turn_da(*steps[last], (0,), nc.scalar.copy)
        second_product(*steps[last - 1], both, False)
        turn_da(*steps[last], (1,), nc.scalar.copy)
        second_product(*steps[last], (0,), False)
        second_product(*steps[last], (1,), False)
